import numpy as np, ml_dtypes
CORES = [9,25,41,57]
N = 4
BF = ml_dtypes.bfloat16
V, H, M, CAP, R = 2560, 160, 1, 64, 5
L = M * H
def lanes(t, r):
    c = (M * (N * t + r) + np.arange(M)) & 15
    return (16 * np.arange(H)[None, :] + c[:, None]).reshape(-1)
def pack(b, x, lm):
    return {"nb": np.ascontiguousarray(b.reshape(N, 128, V)).astype(np.float32), "xs": np.ascontiguousarray(x.reshape(N, 128, V)).astype(np.float32).astype(BF),
            "lim": np.ascontiguousarray(lm.reshape(N, 128, 1)).astype(np.int32)}
def parts(rng):
    dens = rng.choice(np.array([0.08, 0.25, 0.5, 0.8]), (N, 8, 1, V)); u = rng.random((N, 8, 16, V))
    h = np.minimum((V * u * u).astype(np.int64), V - 1)
    pool = rng.integers(V // 4, V, (8, 12)); known = pool[np.arange(8)[None, :, None, None], rng.integers(0, 12, (N, 8, 16, V))]
    h = np.where(rng.random((N, 8, 16, V)) < 0.35, known, h)
    b = np.where(rng.random((N, 8, 16, V)) < dens, h, V)
    top = np.where(rng.random((N, 8, 1, V)) < 0.02, 256, rng.choice(np.array([4, 16, 40, 64]), (N, 8, 1, V)))
    x = (top * rng.random((N, 8, 16, V))).astype(np.int64)
    lm = rng.permutation(np.array([6, 16, 28, 45, 70, 110, 180, 300]))[None, :, None] + rng.integers(0, 8, (N, 8, 16))
    return b, x, lm
def late(rng, b, x, lm, g):
    E = np.stack([np.append(rng.permutation(lanes(0, r)[:-1]), lanes(0, r)[-1])[-26:] for r in range(N)])
    C = np.stack([np.append(rng.permutation(lanes(1, r)[:-1]), lanes(1, r)[-1])[-14:] for r in range(N)])
    D = np.stack([rng.permutation(np.setdiff1d(lanes(2, r), E[r]))[:4] for r in range(N)])
    low = E[:, :12]; own = E[:, 12:18]; top = E[:, 18:]; lows = low.reshape(-1)
    pool = np.setdiff1d(np.arange(V), np.concatenate([E.reshape(-1), C.reshape(-1), D.reshape(-1)]))
    b[:, g] = rng.choice(pool, (N, 16, V)); x[:, g] = rng.integers(128, 256, (N, 16, V)); lm[:, g] = rng.integers(600, 1600, (N, 16))
    for r in range(N):
        b[r, g][:, E[r]] = V; b[r, g][:, C[r, :3]] = V
    for r in range(N):
        z = rng.permutation(pool)[:12]; x[r, g][:, z] = 255; x[r, g][rng.integers(0, 16, 12), z] = 254
        b[r, g][rng.integers(0, 16, 12), low[r]] = z
        p = rng.integers(0, 16, 8); b[r, g][p, top[r]] = rng.choice(pool, 8); b[r, g][(p + rng.integers(1, 16, 8)) & 15, top[r]] = rng.choice(pool, 8)
        q = (r + 1) % N; s = C[r, :6]; k = rng.integers(0, 16, 6); j = (k + rng.integers(1, 16, 6)) & 15
        b[q, g][k, own[q]] = s; b[r, g][k, s] = s; b[r, g][j, s] = own[q]
        for i in range(8):
            n = rng.permutation(lows)[:16]; n[12 + (i & 3)] = top[q, i] if i < 4 else top[0, i]
            b[r, g][:, C[r, 6 + i]] = n
        if r < N - 1:
            for i in range(4):
                n = rng.permutation(lows)[:16]; n[int(rng.integers(0, 16))] = top[0, 4 + i]
                b[r, g][:, D[r, i]] = n
def setup_inputs(rng):
    return pack(*parts(rng))
def setup_inputs_spread(rng):
    d = rng.random((N, 8, 1, V))
    b = np.where(rng.random((N, 8, 16, V)) < d * d * d, rng.integers(0, V, (N, 8, 16, V)), V)
    x = np.minimum((np.exp2(8 * rng.random((N, 8, 1, V))) * rng.random((N, 8, 16, V))).astype(np.int64), 255)
    lm = np.minimum((np.exp2(3 + 9 * rng.random((N, 8, 1))) * (0.5 + 0.5 * rng.random((N, 8, 16)))).astype(np.int64), 4079)
    return pack(b, x, lm)
def setup_inputs_ends(rng):
    x = 255 * np.where(rng.random((N, 8, 1, V)) < 0.5, rng.integers(0, 2, (N, 8, 1, V)), rng.integers(0, 2, (N, 8, 16, V)))
    x[:, 1::2, :, :16] = 255; x[:, 1::2, :, V - 1] = 255
    mode = rng.choice(np.array([0, 0, 1, 2, 2, 2, 3, 4]), (N, 8, 1, V)); coin = rng.integers(0, 2, (N, 8, 16, V))
    v = np.arange(V)[None, :]; p = np.arange(16)[:, None]
    b = np.where(mode == 0, 0, np.where(mode == 1, V, np.where(mode == 2, coin * V, np.where(mode == 3, np.where(coin == 1, p, V - 1), rng.integers(0, V + 1, (N, 8, 16, V))))))
    b[:, 0:6:2, :, 0:16:2] = V
    b[:, 3:6:2, :, 0:16] = V; b[:, 3:6:2, 5, 0:16] = 0
    b[N - 1, 7] = np.where((v >= V - 192) & (p == ((v >> 4) & 15)), V, 0)
    big = np.array([9, 16, 8, 16, 0, 9, 12, 16])[None, :, None]
    lm = np.where(np.argsort(rng.random((N, 8, 16)), axis=2) < big, 4079, 0)
    return pack(b, x, lm)
def setup_inputs_corners(rng):
    x = rng.integers(16, 32, (N, 8, 16, V)); x[..., V - 80:V - 16] = 255; x[..., V - 16:] = 0
    pos = np.argsort(rng.random((N, 8, 16, V)), axis=2)
    many = np.where((rng.random((N, 8, 16, V)) < 0.4) | (pos < 4), rng.integers(0, V - 16, (N, 8, 16, V)), V)
    one = np.where(pos == 0, rng.integers(0, V - 80, (N, 8, 16, V)), V)
    kind = rng.choice(np.array([0, 1, 2, 2]), (N, 8, 1, V)); counts = (CAP, CAP + 1, L, CAP - 1, 1, 0, CAP, 2)
    for q in range(N):
        v = lanes(0, q)
        for g in range(8):
            n = counts[(g + 3 * q) % 8]; o = rng.permutation(L)
            kind[q, g, 0, v[o[:n]]] = 0 if g % 4 == 2 else rng.integers(0, 2, n)
            kind[q, g, 0, v[o[n:]]] = rng.integers(1, 3, L - n) if g % 4 == 2 else 2
    b = np.where(kind == 0, V, np.where(kind == 1, one, many))
    lm = 40 + rng.integers(0, 8, (N, 8, 16)); o = np.argsort(rng.random((N, 8, 16)), axis=2)
    lm[:, 1::2] = np.where(o[:, 1::2] < 9, lm[:, 1::2], 0); lm[:, 2::4] = np.where(o[:, 2::4] < 8, lm[:, 2::4], 0)
    return pack(b, x, lm)
def setup_inputs_crowd(rng):
    b, x, lm = parts(rng)
    b[:, :4] = np.where(rng.random((N, 4, 16, V)) < 0.1, rng.integers(V - 128, V, (N, 4, 16, V)), V); b[:, :4, 0, :] = 0
    v = np.arange(V)
    for t in range(16 // (N * M)):
        c = (M * (N * t + N - 1)) & 15
        b[:, 1:4:2, 0, np.flatnonzero(((v & 15) == c) & ((v >> 4) % CAP == CAP - 1))] = V
    lm[:, :4] = 4079; x[:, :2] = 255
    b[:, 4:] = np.where(b[:, 4:] < V, rng.choice(np.array([0, 1, 18, 40, V - 1]), (N, 4, 16, V)), V); b[:, 4:, :, :48] = V
    return pack(b, x, lm)
def setup_inputs_alike(rng):
    b, x, lm = parts(rng)
    u = rng.random((N, 8, 3, V)); few = np.minimum((V * u * u).astype(np.int64), V - 1)
    few[:, :, 0] = np.where(rng.random((N, 8, V)) < 0.15, np.arange(V), few[:, :, 0])
    pool = rng.integers(V // 2, V, (8, 4)); few[:, :, 2] = pool[np.arange(8)[None, :, None], rng.integers(0, 4, (N, 8, V))]
    which = np.minimum(rng.integers(0, 3, (N, 8, 16, V)), rng.integers(0, 3, (N, 8, 1, V)))
    b = np.where(rng.random((N, 8, 16, V)) < rng.choice(np.array([0.4, 0.8, 1.0]), (N, 8, 1, V)), np.take_along_axis(few, which, 2), V)
    lm = np.minimum(4 * lm, 4079)
    late(rng, b, x, lm, int(rng.integers(0, 8)))
    return pack(b, x, lm)
def check_inputs(d):
    bad = []
    for k, lo, hi in (("nb", 0, V), ("xs", 0, 255), ("lim", 0, 4079)):
        a = np.asarray(d[k]).astype(np.float64)
        if not np.all((a >= lo) & (a <= hi)): bad.append("range of " + k)
        elif not np.all(a == np.floor(a)): bad.append("whole numbers in " + k)
    return bad
def reference(nb, xs, lim):
    b = nb.astype(np.int32).reshape(N, 8, 16, V); x = xs.astype(np.float32).astype(np.int32).reshape(N, 8, 16, V)
    lm = lim.astype(np.int64).reshape(N, 8, 16, 1)
    J = np.tile(np.arange(V), (8, 1)); gone = np.zeros((8, V), bool)
    A = [0] * N; g8 = np.arange(8)[:, None, None]
    for t in range(R):
        new = []
        for r in range(N):
            v = lanes(t, r); q = b[r][:, :, v]
            has = q < V; u = np.where(has, q, 0)
            n = J[g8, u]; elem = has & gone[g8, u]; var = has & ~elem
            at = n.reshape(8, 1, 16 * L)
            Q = np.take_along_axis(b[r], at, 2).reshape(8, 16, 16, L); X = np.take_along_axis(x[r], at, 2).reshape(8, 16, 16, L)
            ek = elem[:, None]
            cov = var & np.any((Q == q[:, :, None, :]) & ek, axis=2)
            unc = var & ~cov
            deg = np.sum(np.where(unc[:, None], X, 0), axis=2) + np.max(np.where(ek, X, 0), axis=2)
            live = ~gone[:, v]
            hit = live & (np.sum(deg <= lm[r] + (A[r] & 7), axis=1) >= 9)
            piv = hit & (np.add.accumulate(hit.astype(np.int64), axis=1) <= CAP)
            col = np.minimum(np.where(unc & (q != v), q, V), np.min(np.where(ek & (Q != v), Q, V), axis=2))
            S = np.where(elem, np.sum(X, axis=1), -1); k = np.argmax(S, axis=1)
            e = np.take_along_axis(n, k[:, None, :], 1)[:, 0, :]
            b[r][:, :, v] = np.where(cov & (live & ~piv)[:, None, :], V, q)
            new.append((v, piv, col, np.minimum(deg, 255), e, piv & np.any(elem, axis=1)))
        for g in range(8):
            es = []; vs = []
            for v, piv, col, sz, e, cl in new:
                w = np.flatnonzero(piv[g]); b[:, g][:, :, v[w]] = col[g][:, w]; x[:, g][:, :, v[w]] = sz[g][:, w]; gone[g, v[w]] = True
                w = np.flatnonzero(cl[g]); es.append(e[g][w]); vs.append(v[w])
            ue, ui = np.unique(np.concatenate(es), return_index=True)
            J[g, ue] = np.concatenate(vs)[ui]
            J[g] = J[g][J[g]]
        A = [int(np.sum(a[1])) for a in new]
    return {"yn": b.reshape(N, 128, V).astype(np.float32), "yx": x.reshape(N, 128, V).astype(np.float32).astype(BF), "yj": np.stack([J] * N).astype(np.float32)}

from concourse.bass import DstId, RemoteDMATransfer
from concourse.mybir import AluOpType, ActivationFunctionType

A = AluOpType
F = ActivationFunctionType
V, N, R = 2560, 4, 5
W = 2640
NT, XT = 3600, 3616
EPS = 2.0 ** -10
SL = 72
LL = 24

SCRATCH = {}
for _d, _spec in (
    ("float32", "NBN:3600 NU:3600 LIMF:1 THR:1 FNA:2640 FNB:2640 L1:1440 L2:1440 QF:640 QN16:640 QM:640 PREA:640 SG:640 VN:640 "
     "QD:160 QPF:160 NE:160 QA:160 QE:2560 QE2:2560 QL:160 OC:160 CODB:160 CODA:160 DEG:160 D1:160 SD:160 U1:10 U2:10 U3:10 "
     "THA:10 THW:10 CW:10 CW1:10 LV:64 LVM:64 LVS:64 DM64:64 TS:1024 EW:4 EO:24 TR4:4 QG:1024 NS:1024 XSA:288 XSS:288 ZERO:64 "
     "YJ:2560 MASKI:256 LANE:160 PREB:160 I16:10 TC:64 IDF:128"),
    ("bfloat16", "XSN:3616 XEA:2640 XEB:2640 SGN:2560 EQ:2560 UNC:2560 XEG:2560 MXS:2560 XVG:2560 NONEL:160 WW:160 CV:160 CV2:160 "
     "AXR:160 LIVE:160 MP:160 OK:160 HX:12 XSC:12 ONES:128 TM:1 AXC:1024 SGC:1024 TF:64 DC:256 DS:256 MM:1024 RM:2560 RN:2560 "
     "R64:256 BIAS:512 MASKJ:256 G1:128 GG:128 TRI:128 ID:128 IDB:128 GS:128 GJ:128 GN:128 BM:2048 JM:2048 DM:2048"),
    ("int32", "LIMI:1 AI:1 AJ:1 QI:160 QI2:160 QI3:160 CA:320 CB:320 CBI:64 C1:64 C2:64 C3:64 C4:64 TI:64 TB:64 EXPI:160 TCI:16"),
    ("uint16", "JL:160 L3:480 QPU:640 QLU:160 SLU:10 QCU:64 EXPL:160"),
):
    for _e in _spec.split():
        SCRATCH[_e.split(":")[0]] = ("sbuf", [128, int(_e.split(":")[1])], _d)
for _e in "pD pE pC pM pW pN0 pN1".split():
    SCRATCH[_e] = ("psum", [128, 512], "float32")
SEMAPHORES = ["v", "s", "t", "p", "lo", "d_nb0", "d_nb1", "d_xs", "d_lim", "d_yn", "d_yx", "d_yj"] + [
    "a%d_%d_%d" % (k, t, q) for k in (1, 2, 3) for t in range(R) for q in range(N)]


def queues(g, T):
    eng = {"v": g.vector, "s": g.scalar, "t": g.tensor, "p": g, "y": g.sync}
    cnt = {"v": 0, "s": 0, "t": 0, "p": 0}
    know = {q: {} for q in eng}
    lastw, readers, dmas = {}, {}, {}

    def wait(q, tok):
        sem, val, clock, _ = tok
        if know[q].get(sem, 0) < val:
            eng[q].wait_ge(T.sem[sem], val)
            know[q][sem] = val
        for k, n in clock.items():
            if know[q].get(k, 0) < n:
                know[q][k] = n

    def before(q, R_, W_):
        toks = [lastw[k] for k in R_ if k in lastw]
        for k in W_:
            toks += [x for x in list(readers.get(k, {}).values()) + ([lastw[k]] if k in lastw else [])
                     if not (x[3] == q and q == "t")]
        for tok in sorted(toks, key=lambda x: -x[1]):
            wait(q, tok)

    def after(tok, R_, W_):
        for k in W_:
            lastw[k] = tok
            readers[k] = {}
        for k in R_:
            readers.setdefault(k, {})[tok[0]] = tok

    def op(q, fns, R_=(), W_=()):
        before(q, R_, W_)
        for f in (fns if isinstance(fns, list) else [fns]):
            ins = f()
        cnt[q] += 1
        ins.then_inc(T.sem[q], 1)
        after((q, cnt[q], dict(know[q]), q), R_, W_)

    def dma(q, sem, fns, R_=(), W_=()):
        before(q, R_, W_)
        for f in fns:
            dmas[sem] = dmas.get(sem, 0) + 16
            f().then_inc(T.sem[sem], 16)
        after((sem, dmas[sem], dict(know[q]), "dma"), R_, W_)

    def arrive(sem, n, W_):
        dmas[sem] = n
        after((sem, n, {}, "far"), (), W_)

    def finish(extra):
        for sem, n in list(cnt.items()) + list(dmas.items()) + extra:
            if n and know["y"].get(sem, 0) < n:
                g.sync.wait_ge(T.sem[sem], n)

    return op, dma, arrive, finish, before


def rank_program(g, core, T, topo):
    r = T.rank_of(core)
    if r is None:
        return
    vec, sca, ten = g.vector, g.scalar, g.tensor
    op, dma, arrive, finish, before = queues(g, T)
    others = [d for d in T.cores if d != core]

    def cp(out, in_, R_, W_):
        op("v", lambda: vec.tensor_copy(out=out, in_=in_), R_, W_)

    def tt(out, a, b, o, R_, W_):
        op("v", lambda: vec.tensor_tensor(out=out, in0=a, in1=b, op=o), R_, W_)

    def ts(out, a, s1, o1, s2, o2, R_, W_):
        if o2 is None:
            op("v", lambda: vec.tensor_scalar(out=out, in0=a, scalar1=s1, scalar2=None, op0=o1), R_, W_)
        else:
            op("v", lambda: vec.tensor_scalar(out=out, in0=a, scalar1=s1, scalar2=s2, op0=o1, op1=o2), R_, W_)

    def scan(out, d0, d1, o0, o1, R_, W_):
        op("v", lambda: vec.tensor_tensor_scan(out=out, data0=d0, data1=d1, initial=0.0, op0=o0, op1=o1), R_, W_)

    def fill(ap, x, W_):
        op("v", lambda: vec.memset(ap, x), (), W_)

    def act(out, in_, R_, W_, func=F.Copy, **kw):
        op("s", lambda: sca.activation(out, in_, func, **kw), R_, W_)

    def iota(out, pattern, base, cm, W_):
        op("p", lambda: g.iota(out, pattern, base, cm, allow_small_or_imprecise_dtypes=True), (), W_)

    def mm(out, l, rr, st, sp):
        return lambda: ten.matmul(out, l, rr, st, sp)

    def tab(name, a, b, *more):
        return [(name, x) for x in range(a, b)] + [(name, x) for x in more]

    def whole(name):
        return tab(name, 0, 16, "n")
    M16 = range(16)
    NB, XS = ["NB0", "NB1"], ["XS", "XS0"]
    BMk, DMk = [("BM", m) for m in M16], [("DM", m) for m in M16]

    dma("y", "d_nb0", [lambda: g.sync.dma_start(T.NBN[:, 0:1280], T.nb[:, 0:1280])], (), ["NB0"])
    dma("s", "d_nb1", [lambda: g.scalar.dma_start(T.NBN[:, 1280:2560], T.nb[:, 1280:2560])], (), ["NB1"])
    dma("y", "d_xs", [lambda: g.sync.dma_start(T.XSN[:, 16:2576], T.xs[:])], (), ["XS"])
    dma("s", "d_lim", [lambda: g.scalar.dma_start(T.LIMI[:], T.lim[:])], (), ["LIMI"])

    iota(T.TCI[:, 0:1], [[1, 1]], 0, 1, ["TCI"])
    iota(T.LANE[:], [[1, 160]], 0, 0, ["LANE"])
    fill(T.ONES[:], 1.0, ["ONES"])
    ones = T.ONES[:]
    op("p", lambda: g.affine_select(T.ID[:], ones, [[-1, 128]], A.is_equal, 0.0, 0, 1), ["ONES"], ["ID"])
    op("p", lambda: g.affine_select(T.G1[:], ones, [[-16, 8], [0, 16]], A.is_ge, 0.0, 0, 1), ["ONES"], ["G1"])
    op("p", lambda: g.affine_select(T.GG[:], T.G1[:], [[16, 8], [0, 16]], A.is_ge, 0.0, 15, -1), ["G1"], ["GG"])
    iota(T.I16[:], [[16, 10]], 0, 0, ["I16"])
    op("p", lambda: g.affine_select(T.TRI[:], T.GG[:], [[1, 128]], A.is_ge, 0.0, 0, -1), ["GG"], ["TRI"])
    iota(T.EXPI[:], [[1, 160]], 0, 0, ["EXPI"])
    iota(T.CBI[:], [[1, 64]], 2560 * 256 + 161, 0, ["CBI"])
    iota(T.TC[:, 40:44], [[16, 4]], 2576, 0, ["T40"])
    iota(T.LVM[:], [[0, 4], [1, 16]], 0, 0, ["LVM"])
    iota(T.MASKI[:], [[-16, 4], [1, 64]], 0, 0, ["MASKI"])
    iota(T.BIAS[:], [[0, 32], [-4, 16]], 61, 0, ["BIAS"])
    iota(T.FNA[:], [[0, W]], V, 0, whole("FNA"))
    iota(T.NU[:, 0:V], [[1, V]], 0, 0, ["NU"])
    fill(T.XSN[:, 0:16], 0.0, ["XS0"])
    fill(T.XSN[:, 2576:2592], 0.0, ["XS0"])
    fill(T.BM[:], 0.0, BMk)
    fill(T.DM[:], 0.0, DMk)
    for m in M16:
        act(T.BM[:, 128 * m + m:128 * m + 128:16], T.GG[:, m:128:16], ["GG"], [("BM", m)])
    for m in M16:
        act(T.DM[:, 128 * m + m:128 * m + 128:16], T.ID[:, m:128:16], ["ID"], [("DM", m)])
    ts(T.TCI[:, 1:2], T.TCI[:, 0:1], 15, A.bitwise_and, None, None, ["TCI"], ["TCI1"])
    for b in range(4):
        ts(T.TCI[:, 4 + b:5 + b], T.TCI[:, 1:2], b, A.logical_shift_right, 1, A.bitwise_and, ["TCI1"], ["TCB%d" % b])
    cp(T.TC[:, 0:1], T.TCI[:, 1:2], ["TCI1"], ["PM"])
    for b in range(4):
        up = float(2 ** (2 ** b))
        ts(T.TC[:, 12 + b:13 + b], T.TCI[:, 4 + b:5 + b], up - 1.0, A.mult, 1.0, A.add, ["TCB%d" % b], ["UP%d" % b])
        ts(T.TC[:, 16 + b:17 + b], T.TCI[:, 4 + b:5 + b], 1.0 / up - 1.0, A.mult, 1.0, A.add, ["TCB%d" % b], ["DN%d" % b])
    for nm, c0, d in (("UP", 12, 1), ("DN", 16, 2)):
        tt(T.TC[:, 20 + d:21 + d], T.TC[:, c0:c0 + 1], T.TC[:, c0 + 1:c0 + 2], A.mult, [nm + "0", nm + "1"], [nm + "a"])
        tt(T.TC[:, 24 + d:25 + d], T.TC[:, c0 + 2:c0 + 3], T.TC[:, c0 + 3:c0 + 4], A.mult, [nm + "2", nm + "3"], [nm + "b"])
        tt(T.TC[:, d:d + 1], T.TC[:, 20 + d:21 + d], T.TC[:, 24 + d:25 + d], A.mult, [nm + "a", nm + "b"], [nm])
    pm, up, dn = T.TC[:, 0:1], T.TC[:, 1:2], T.TC[:, 2:3]
    cp(T.EXPL[:], T.EXPI[:], ["EXPI"], ["EXPL"])
    ts(T.PREB[:], T.LANE[:], float(2560 * 256), A.add, None, None, ["LANE"], ["PREB"])

    def signs(k):
        c = 4 * k + r
        s = slice(160 * k, 160 * k + 160)
        ts(T.QD[:], T.LANE[:], float(256 * (15 - c)), A.add, None, None, ["LANE"], ["QD"])
        ts(T.VN[:, s], T.LANE[:], 16.0, A.mult, float(c), A.add, ["LANE"], ["VN%d" % k])
        ts(T.QPF[:], T.QD[:], dn, A.mult, -0.495, A.add, ["QD", "DN"], ["QPF"])
        cp(T.QI[:], T.QPF[:], ["QPF"], ["QI"])
        ts(T.QI2[:], T.QI[:], 1, A.bitwise_and, None, None, ["QI"], ["QI2"])
        ts(T.SG[:, s], T.QI2[:], 2.0, A.mult, -1.0, A.add, ["QI2"], ["SG%d" % k])
    for k in range(4):
        signs(k)
    ts(T.TC[:, 8:9], pm, 7.5, A.is_lt, 0.5, A.mult, ["PM"], ["W0"])
    ts(T.TC[:, 9:10], pm, 11.5, A.is_lt, 0.5, A.mult, ["PM"], ["W1"])
    ts(T.TC[:, 10:11], pm, 12.0, A.is_equal, None, None, ["PM"], ["W2"])
    ts(T.TC[:, 11:12], pm, 13.0, A.is_equal, -2040.0, A.mult, ["PM"], ["W3"])
    tt(T.TC[:, 28:29], T.TC[:, 8:9], up, A.mult, ["W0", "UP"], ["W4"])
    tt(T.TC[:, 29:30], T.TC[:, 9:10], up, A.mult, ["W1", "UP"], ["W5"])
    ts(T.TC[:, 45:46], T.TC[:, 10:11], 2.0 * EPS, A.mult, -EPS, A.add, ["W2"], ["NX"])
    ts(T.TC[:, 32:33], T.TC[:, 10:11], 1280.0, A.mult, None, None, ["W2"], ["W8"])
    tt(T.TC[:, 30:31], T.TC[:, 29:30], T.TC[:, 28:29], A.subtract, ["W4", "W5"], ["W6"])
    ts(T.TC[:, 37:38], T.TC[:, 10:11], -7.5, A.mult, None, None, ["W2"], ["WC"])
    ts(T.TC[:, 35:36], T.TC[:, 28:29], 16.0, A.mult, None, None, ["W4"], ["WA"])
    ts(T.TC[:, 31:32], T.TC[:, 30:31], 160.0 / 256.0, A.mult, None, None, ["W6"], ["W7"])
    ts(T.TC[:, 36:37], T.TC[:, 30:31], -1.0 / 256.0, A.mult, None, None, ["W6"], ["WB"])
    tt(T.TC[:, 39:40], T.TC[:, 37:38], T.TC[:, 11:12], A.add, ["WC", "W3"], ["WE"])
    tt(T.TC[:, 33:34], T.TC[:, 31:32], T.TC[:, 28:29], A.add, ["W7", "W4"], ["W9"])
    tt(T.TC[:, 38:39], T.TC[:, 35:36], T.TC[:, 36:37], A.add, ["WA", "WB"], ["WD"])
    tt(T.TC[:, 34:35], T.TC[:, 33:34], T.TC[:, 32:33], A.add, ["W8", "W9"], ["WJ"])
    tt(T.TC[:, 44:45], T.TC[:, 38:39], T.TC[:, 39:40], A.add, ["WD", "WE"], ["WN"])
    nx = T.TC[:, 45:46]
    ts(T.CW1[:], T.I16[:], pm, A.add, 160.0, A.add, ["I16", "PM"], ["CW1"])
    ts(T.CW[:], T.CW1[:], 1.0, A.add, None, None, ["CW1"], ["CW"])
    fill(T.HX[:], 0.0, ["HX"])
    fill(T.RM[:], 1.0, ["RM"])
    fill(T.RM[:, 0:2560:16], 0.0, ["RM"])
    fill(T.CA[:, 0:64], V * 1024 + 512, ["CA"])
    cp(T.CB[:, 0:64], T.CBI[:], ["CBI"], ["CB"])
    cp(T.LIMF[:], T.LIMI[:], ["LIMI"], ["LIMF"])
    cp(T.THR[:], T.LIMF[:], ["LIMF"], ["THR"])

    made = []

    def own_s1(k):
        s = slice(160 * k, 160 * k + 160)
        if k not in made:
            act(T.QF[:, s], T.NBN[:, 4 * k + r:V:16], NB, ["QF%d" % k])
            act(T.QA[:], T.QF[:, s], ["QF%d" % k], ["QA"], scale=256.0, bias=-655360.0)
        made.append(k)

    def own_v1(k):
        s = slice(160 * k, 160 * k + 160)
        tt(T.NE[:], T.QF[:, s], T.VN[:, s], A.not_equal, ["QF%d" % k, "VN%d" % k], ["NE"])
        tt(T.QM[:, s], T.QA[:], T.NE[:], A.mult, ["QA", "NE"], ["QM%d" % k])

    def own_v2(k):
        s = slice(160 * k, 160 * k + 160)
        cp(T.QI[:], T.QF[:, s], ["QF%d" % k], ["QI"])
        ts(T.QI2[:], T.QI[:], 15, A.bitwise_and, None, None, ["QI"], ["QI2"])
        ts(T.QI3[:], T.QI[:], 4, A.logical_shift_right, None, None, ["QI"], ["QI3"])
        ts(T.QD[:], T.QI2[:], -160.0, A.mult, 2400.0, A.add, ["QI2"], ["QD"])
        tt(T.QPF[:], T.QD[:], T.QI3[:], A.add, ["QD", "QI3"], ["QPF"])
        cp(T.QPU[:, s], T.QPF[:], ["QPF"], ["QPU%d" % k])

    def own_s2(k):
        s = slice(160 * k, 160 * k + 160)
        act(T.QN16[:, s], T.QF[:, s], ["QF%d" % k], ["QN%d" % k], bias=16.0)
        act(T.PREA[:, s], T.QPF[:], ["QPF"], ["PREA%d" % k], scale=1024.0, bias=512.0)

    def expand(k, name, h):
        act(T[name][:, 1280 * h:1280 * h + 1280], T.QF[:, 160 * k:160 * k + 160].indirect(T.EXPL[:, 80 * h:80 * h + 80]),
            ["QF%d" % k, "EXPL"], [name + str(h)])

    mask = topo.mask(core, others[0])
    for d in others:
        mask &= topo.mask(core, d)
    neng = len([e for e in topo.engines(core, others[0]) if mask >> e & 1])
    ids = [DstId(rid=topo.addr(d)[0], pnc=topo.addr(d)[1]) for d in others]
    nsend = [0]

    def send(kind, t, buf, w, n):
        ap = T[buf][:, (4 * t + r) * w:(4 * t + r) * w + n]
        before("p", [(buf, t, r)], ())
        g.remote_dma_fused([RemoteDMATransfer(dst_ids=ids, dma_engine_mask=mask, remote_sem=T.sem["a%d_%d_%d" % (kind, t, r)],
                                              srcs=[ap], dsts=[ap for d in others])], local_sem=T.sem["lo"])
        nsend[0] += neng
    for t in range(R):
        for q in range(N):
            if q != r:
                for kind, buf in ((1, "L1"), (2, "L2"), (3, "L3")):
                    arrive("a%d_%d_%d" % (kind, t, q), neng, [(buf, t, q)])

    def l1(t, q, a=0, b=64):
        return T.L1[:, (4 * t + q) * SL + a:(4 * t + q) * SL + b]

    def l2(t, q, a=0, b=64):
        return T.L2[:, (4 * t + q) * SL + a:(4 * t + q) * SL + b]

    def l3(t, q, a, b):
        return T.L3[:, (4 * t + q) * LL + a:(4 * t + q) * LL + b]

    def keep_sizes(t):
        act(T.XSA[:], T.L1[:, 4 * t * SL:4 * (t + 1) * SL], [("L1", t, q) for q in range(N)], ["XSA"], func=F.Abs)
        act(T.XSS[:], T.XSA[:], ["XSA"], ["XSS"], bias=-1.0)

    def store_sizes(t):
        for q in range(N):
            cp(T.XSN[:, 16:XT].indirect(l3(t, q, 14, 18)), T.XSS[:, SL * q:SL * q + 64], ["XSS", ("L3", t, q)], XS)

    def store_names(t):
        for q in range(N):
            cp(T.NBN[:, 0:NT].indirect(l3(t, q, 14, 18)), l2(t, q), [("L2", t, q), ("L3", t, q)], NB)

    def store_gone(t):
        for q in range(N):
            cp(T.NU[:, 0:NT].indirect(l3(t, q, 14, 18)), T.ZERO[:], ["ZERO", ("L3", t, q)], ["NU"])

    PARTS = ((0, 48, "s"), (48, 96, "s"), (96, 160, "v"))
    ts(T.QLU[:], T.NBN[:, r:V:16], 16.0, A.add, None, None, NB, ["QLU"])

    cur, nxt = "A", "B"
    for t in range(R):
        k = t % 4
        k1 = (t + 1) % 4
        ks = slice(160 * k, 160 * k + 160)
        lo = 640 * (4 - t)
        n = V - lo
        fn, xe = T["FN" + cur], T["XE" + cur]
        qe, qe1 = ("QE", "QE2") if t % 2 else ("QE2", "QE")
        FNk, XEk = whole("FN" + cur), whole("XE" + cur)
        if t:
            for h in range(2):
                s, l = slice(1280 * h, 1280 * h + 1280), T.QPU[:, 160 * k + 80 * h:160 * k + 80 * h + 80]
                act(T.XEG[:, s], xe[:, 0:2576].indirect(l), XEk + ["QPU%d" % k], ["XEG%d" % h], func=F.Abs)
                tt(T.EQ[:, s], fn[:, 0:2576].indirect(l), T[qe][:, s], A.not_equal, FNk + ["QPU%d" % k, qe + str(h)], ["EQ%d" % h])
                op("t", [mm(T.pE[:, 80 * h:80 * h + 80], T.DM[:, 128 * j:128 * j + 128], T.XEG[:, 1280 * h + j:1280 * h + 1280:16],
                            j == 0, j == 15) for j in M16], DMk + ["XEG%d" % h], ["pE"])
            scan(T.UNC[:], T.RN[:], T.EQ[:], A.max, A.min, ["RN", "EQ0", "EQ1"], ["UNC"])
            ts(T.NONEL[:], T.pE[:, 0:160], 0.5, A.is_lt, None, None, ["pE"], ["NONEL"])
            tt(T.WW[:], T.UNC[:, 15:V:16], T.NONEL[:], A.mult, ["UNC", "NONEL"], ["WW"])
            tt(T.QL[:], T.QN16[:, ks], T.WW[:], A.mult, ["QN%d" % k, "WW"], ["QL"])
            cp(T.QLU[:], T.QL[:], ["QL"], ["QLU"])
        for a, b, q in PARTS:
            o, i = T.XVG[:, 16 * a:16 * b], T.XSN[:, 0:2592].indirect(T.QLU[:, a:b])
            if q == "s":
                act(o, i, XS + ["QLU"], ["XVG%d" % a])
            else:
                cp(o, i, XS + ["QLU"], ["XVG%d" % a])
        for a, b, q in (PARTS[0], PARTS[2], PARTS[1]):
            op("t", [mm(T.pD[:, a:b], T.ID[:], T.XVG[:, 16 * a + j:16 * b:16], j == 0, j == 15) for j in M16],
               ["ID", "XVG%d" % a], ["pD"])
        if t:
            scan(T.MXS[:], T.RM[:], T.XEG[:], A.mult, A.max, ["RM", "XEG0", "XEG1"], ["MXS"])
            tt(T.OC[:], T.QM[:, ks], T.WW[:], A.mult, ["QM%d" % k, "WW"], ["OC"])
            ts(T.MP[:], T.MXS[:, 15:V:16], 1.0, A.max, 1.0, A.subtract, ["MXS"], ["MP"])
            tt(T.CODB[:], T.OC[:], T.PREB[:], A.add, ["OC", "PREB"], ["CODB"])
            if t >= 2:
                act(T.SGN[:, lo:V], xe[:, lo:V], tab("XE" + cur, lo // 160, 16), ["SGN"], func=F.Sign)
            if t < 4:
                own_s1(k1)
                expand(k1, qe1, 0)
            tt(T.DEG[:], T.pD[:, 0:160], T.MP[:], A.add, ["pD", "MP"], ["DEG"])
        else:
            own_s1(0)
            own_v1(0)
            tt(T.CODB[:], T.QM[:, ks], T.PREB[:], A.add, ["QM0", "PREB"], ["CODB"])
            act(T.XEA[:], T.FNA[:], whole("FNA") + ["NX"], whole("XEA"), func=F.Identity, scale=0.0, bias=nx)
            own_s1(1)
            expand(1, qe1, 0)
            expand(1, qe1, 1)
            ts(T.DM64[:], T.LVM[:], pm, A.is_equal, None, None, ["LVM", "PM"], ["DM64"])
            ts(T.TR4[:], T.TC[:, 40:44], pm, A.add, None, None, ["T40", "PM"], ["TR4"])
            fill(T.ZERO[:], 0.0, ["ZERO"])
            cp(T.DEG[:], T.pD[:, 0:160], ["pD"], ["DEG"])
        ts(T.OK[:], T.DEG[:], T.THR[:], A.is_le, None, None, ["DEG", "THR"], ["OK"])
        op("t", [mm(T.pC[:, 0:10], T.BM[:, 128 * m:128 * m + 128], T.OK[:, m:160:16], m == 0, m == 15) for m in M16], BMk + ["OK"], ["pC"])
        ts(T.D1[:], T.DEG[:], 255.0, A.min, 1.0, A.add, ["DEG"], ["D1"])
        tt(T.SD[:], T.D1[:], T.SG[:, ks], A.mult, ["D1", "SG%d" % k], ["SD"])
        if t:
            tt(T.CODA[:], T.SD[:], T.PREA[:, ks], A.add, ["SD", "PREA%d" % k], ["CODA"])
        else:
            ts(T.CODA[:], T.SD[:], 512.0, A.add, None, None, ["SD"], ["CODA"])
        if t < 4:
            ts(T.HX[:, 1:11], T.pC[:, 0:10], 8.5, A.is_ge, None, None, ["pC"], ["HX"])
        else:
            tt(T.HX[:, 1:11], T.pC[:, 0:10], T.THW[:], A.is_ge, ["pC", "THW"], ["HX"])
        scan(T.XSC[:, 0:11], T.ONES[:, 0:11], T.HX[:, 0:11], A.mult, A.add, ["ONES", "HX"], ["XSC"])
        op("t", [mm(T.pC[:, 16:26], T.TRI[:], T.HX[:, 1:11], True, False), mm(T.pC[:, 16:26], T.GG[:], T.XSC[:, 0:10], False, True),
                 mm(T.pC[:, 32:33], T.GG[:], T.XSC[:, 10:11], True, True)], ["TRI", "GG", "HX", "XSC"], ["pC"])
        tt(T.U1[:], T.pC[:, 16:26], T.CW[:], A.subtract, ["pC", "CW"], ["U1"])
        tt(T.U2[:], T.U1[:], T.HX[:, 1:11], A.mult, ["U1", "HX"], ["U2"])
        tt(T.U3[:], T.U2[:], T.CW1[:], A.add, ["U2", "CW1"], ["U3"])
        cp(T.SLU[:], T.U3[:], ["U3"], ["SLU"])
        L1k, L2k, L3k = ("L1", t, r), ("L2", t, r), ("L3", t, r)
        cp(T.CA[:, 0:320].indirect(T.SLU[:]), T.CODA[:], ["SLU", "CODA"], ["CA"])
        if t:
            if t >= 2:
                op("t", [mm(T.pW[:, 16:16 + n // 16], T.JM[:, 128 * m:128 * m + 128], T.SGN[:, lo + m:V:16], m == 0, m == 15) for m in M16],
                   ["JM", "SGN"], ["pW"])
            ts(T.C1[:], T.CA[:, 0:64], 10, A.logical_shift_right, None, None, ["CA"], ["C1"])
            cp(T.QCU[:], T.C1[:], ["C1"], ["QCU"])
            hs = [(b, slice(512 * b, 512 * b + 512), T.QCU[:, 32 * b:32 * b + 32]) for b in range(2)]
            for b, s, l in hs:
                act(T.QG[:, s], fn[:, 0:2576].indirect(l), FNk + ["QCU"], ["QG%d" % b])
                op("t", mm(T["pN%d" % b][:], T.IDF[:], T.QG[:, s], True, False), ["IDF", "QG%d" % b], ["pN%d" % b])
            for b, s, l in hs:
                bank = ("pD", "pE")[b]
                act(T.AXC[:, s], xe[:, 0:2576].indirect(l), XEk + ["QCU"], ["AXC%d" % b], func=F.Abs)
                act(T.SGC[:, s], xe[:, 0:2576].indirect(l), XEk + ["QCU"], ["SGC%d" % b], func=F.Sign)
                op("t", [mm(T[bank][:], T.ID[:], T.BIAS[:], True, False), mm(T[bank][:], T.GS[:], T.AXC[:, s], False, False),
                         mm(T[bank][:], T.ID[:], T.SGC[:, s], False, True)], ["ID", "BIAS", "SGC%d" % b, "GS", "AXC%d" % b], [bank])
        ts(T.C2[:], T.CA[:, 0:64], 1023, A.bitwise_and, None, None, ["CA"], ["C2"])
        ts(l1(t, r), T.C2[:], 512.0, A.subtract, None, None, ["C2"], [L1k])
        ts(l1(t, r, 64, SL), T.BIAS[:, 0:8], 0.0, A.mult, nx, A.add, ["BIAS", "NX"], [L1k])
        send(1, t, "L1", SL, SL)
        cp(T.CB[:, 0:320].indirect(T.SLU[:]), T.CODB[:], ["SLU", "CODB"], ["CB"])
        fill(l2(t, r, 64, SL), float(V), [L2k])
        ts(T.C3[:], T.CB[:, 0:64], 8, A.logical_shift_right, None, None, ["CB"], ["C3"])
        ts(T.C4[:], T.CB[:, 0:64], 255, A.bitwise_and, None, None, ["CB"], ["C4"])
        if t == 0:
            cp(l2(t, r), T.C3[:], ["C3"], [L2k])
            send(2, t, "L2", SL, SL)
        ts(T.LV[:], T.C4[:], 16.0, A.mult, float(4 * k + r), A.add, ["C4"], ["LV"])
        ts(l3(t, r, 4, 14), T.U3[:], 64.0, A.min, None, None, ["U3"], [L3k])
        if t:
            for b, s, l in hs:
                tt(T.MM[:, s], T.LV[:, 0:64].indirect(T.EXPL[:, 32 * b:32 * b + 32]), T.QG[:, s], A.is_equal, ["LV", "EXPL", "QG%d" % b], ["MM%d" % b])
                op("t", mm(T["pN%d" % b][:], T.IDB[:], T.MM[:, s], False, True), ["IDB", "MM%d" % b], ["pN%d" % b])
        tt(T.LVM[:], T.LV[:], T.DM64[:], A.mult, ["LV", "DM64"], ["LVM"])
        scan(T.LVS[:], T.RM[:, 0:64], T.LVM[:], A.mult, A.add, ["RM", "LVM"], ["LVS"])
        cp(l3(t, r, 14, 18), T.LVS[:, 15:64:16], ["LVS"], [L3k])
        if t == 0:
            ts(l3(t, r, 0, 4), T.TR4[:], 0.0, A.mult, None, None, ["TR4"], [L3k])
            send(3, t, "L3", LL, 18)
        else:
            if t < 4:
                if k1:
                    own_v1(k1)
                own_v2(k1)
            store_gone(t - 1)
            for b in range(2):
                bank = ("pD", "pE")[b]
                scan(T.TS[:, 512 * b:512 * b + 512], T.RM[:, 0:512], T[bank][:], A.mult, A.max, ["RM", bank], ["TS%d" % b])
            cp(T.TI[:], T.TS[:, 15:1024:16], ["TS0", "TS1"], ["TI"])
            ts(T.TB[:], T.TI[:], 2, A.bitwise_and, None, None, ["TI"], ["TB"])
            cp(T.TF[:], T.TB[:], ["TB"], ["TF"])
            op("t", [mm(T.pC[:, 48:52], T.JM[:, 128 * m:128 * m + 128], T.TF[:, m:64:16], m == 0, m == 15) for m in M16], ["JM", "TF"], ["pC"])
            op("t", [mm(T.pM[:, 0:256], T.ID[:], T.MASKJ[:], True, False)] +
               [mm(T.pM[:, 64 * s:64 * s + 64], T.GJ[:], T.TF[:], False, s == 3) for s in range(4)], ["ID", "MASKJ", "GJ", "TF"], ["pM"])
            for b in range(2):
                scan(T.NS[:, 512 * b:512 * b + 512], T.RN[:, 0:512], T["pN%d" % b][:], A.max, A.min, ["RN", "pN%d" % b], ["NS%d" % b])
            tt(l2(t, r), T.NS[:, 15:1024:16], T.C3[:], A.min, ["NS0", "NS1", "C3"], [L2k])
            send(2, t, "L2", SL, SL)
            tt(T.CV[:], T.NONEL[:], T.WW[:], A.subtract, ["NONEL", "WW"], ["CV"])
            cp(T.EW[:], T.pC[:, 48:52], ["pC"], ["EW"])
            for s in range(4):
                ts(T.DC[:, 64 * s:64 * s + 64], T.pM[:, 64 * s:64 * s + 64], T.EW[:, s:s + 1], A.is_equal, 4096.0, A.mult, ["pM", "EW"], ["DC%d" % s])
            scan(T.DS[:], T.R64[:], T.DC[:], A.mult, A.max, ["R64"] + ["DC%d" % s for s in range(4)], ["DS"])
            tt(T.EO[:, 0:4], T.DS[:, 63:256:64], T.EW[:], A.add, ["DS", "EW"], ["EO0"])
            ts(T.EO[:, 4:8], T.EO[:, 0:4], 2559.5, A.is_lt, None, None, ["EO0"], ["EO1"])
            tt(T.EO[:, 8:12], T.EO[:, 0:4], T.TR4[:], A.subtract, ["EO0", "TR4"], ["EO2"])
            tt(T.EO[:, 12:16], T.EO[:, 8:12], T.EO[:, 4:8], A.mult, ["EO1", "EO2"], ["EO3"])
            tt(T.EO[:, 16:20], T.EO[:, 12:16], T.TR4[:], A.add, ["EO3", "TR4"], ["EO4"])
            ts(l3(t, r, 0, 4), T.EO[:, 16:20], float(lo), A.subtract, None, None, ["EO4"], [L3k])
            send(3, t, "L3", LL, 18)
        if t < 4:
            ts(T.TM[:], T.pC[:, 32:33], 64.0, A.min, None, None, ["pC"], ["TM"])
            op("t", mm(T.pC[:, 40:41], T.ONES[:], T.TM[:], True, True), ["ONES", "TM"], ["pC"])
            if t == 0:
                own_v1(1)
                own_v2(1)
            own_s2(k1)
            ts(T.AI[:], T.pC[:, 40:41], 1.0 / 16.0, A.mult, None, None, ["pC"], ["AI"])
            ts(T.AJ[:], T.AI[:], 7, A.bitwise_and, None, None, ["AI"], ["AJ"])
            tt(T.THR[:], T.LIMF[:], T.AJ[:], A.add, ["LIMF", "AJ"], ["THR"])
            fill(T.CA[:, 0:64], V * 1024 + 512, ["CA"])
            cp(T.CB[:, 0:64], T.CBI[:], ["CBI"], ["CB"])
        if t == 0:
            ts(T.THA[:], T.U3[:], 63.5, A.is_lt, 100.0, A.mult, ["U3"], ["THA"])
            ts(T.THW[:], T.THA[:], 8.5, A.max, None, None, ["THA"], ["THW"])
            iota(T.FNB[:], [[0, W]], V, 0, whole("FNB"))
            fill(T.RN[:], 0.0, ["RN"])
            fill(T.RN[:, 0:2560:16], 8192.0, ["RN"])
            ts(T.JM[:], T.BM[:], T.TC[:, 34:35], A.mult, None, None, BMk + ["WJ"], ["JM"])
            ts(T.GJ[:], T.GG[:], T.TC[:, 34:35], A.mult, None, None, ["GG", "WJ"], ["GJ"])
            ts(T.GN[:], T.GG[:], T.TC[:, 44:45], A.mult, None, None, ["GG", "WN"], ["GN"])
            ts(T.GS[:], T.GG[:], 64.0, A.mult, None, None, ["GG"], ["GS"])
            ts(T.IDB[:], T.ID[:], 4096.0, A.mult, None, None, ["ID"], ["IDB"])
            cp(T.IDF[:], T.ID[:], ["ID"], ["IDF"])
            ts(T.MASKJ[:], T.MASKI[:], pm, A.is_ge, 8192.0, A.mult, ["MASKI", "PM"], ["MASKJ"])
            fill(T.R64[:], 1.0, ["R64"])
            fill(T.R64[:, 0:256:64], 0.0, ["R64"])
        else:
            if t < 4:
                expand(k1, qe1, 1)
            if t == 1:
                act(T.XEB[:], T.FNB[:], whole("FNB") + ["NX"], whole("XEB"), func=F.Identity, scale=0.0, bias=nx)
            if t >= 2:
                ts(T.JL[:, lo // 16:160], T.pW[:, 16:16 + n // 16], 2607.5, A.add, None, None, ["pW"], ["JL"])
            if t == 4:
                cl = 160 * (15 - r)
                act(T.AXR[:], xe[:, cl:cl + 160], [("XE" + cur, 15 - r)], ["AXR"], func=F.Abs)
                ts(T.LIVE[:], T.AXR[:], 0.5, A.is_lt, None, None, ["AXR"], ["LIVE"])
                tt(T.CV[:], T.CV[:], T.LIVE[:], A.mult, ["CV", "LIVE"], ["CV"])
            ts(T.CV2[:], T.CV[:], float(V), A.mult, None, None, ["CV"], ["CV2"])
            col = T.NBN[:, 4 * k + r:V:16]
            tt(col, col, T.CV2[:], A.max, NB + ["CV2"], NB)
            keep_sizes(t - 1)
            store_sizes(t - 1)
            store_names(t - 1)
        b0 = lo // 160
        wx, wf = tab("XE" + cur, b0, 16, "n"), tab("FN" + cur, b0, 16, "n")
        if t < 4:
            to = nxt if t >= 2 else cur
            if t:
                for q in (3, 2, 1, 0):
                    cp(xe[:, lo:W].indirect(l3(t, q, 0, 4)), l1(t, q), [("L1", t, q), ("L3", t, q)], wx)
            for buf, nm, ld in (("L1", "XE", l1), ("L2", "FN", l2)):
                for q in range(N):
                    bk = 15 - 4 * t - q
                    act(T[nm + to][:, 160 * bk:160 * bk + 160], ld(t, q, 0, SL).indirect(l3(t, q, 4, 14)), [(buf, t, q), ("L3", t, q)], [(nm + to, bk)])
            if t:
                for q in (3, 2, 1, 0):
                    cp(fn[:, lo:W].indirect(l3(t, q, 0, 4)), l2(t, q), [("L2", t, q), ("L3", t, q)], wf)
            if t >= 2:
                act(T["XE" + to][:, lo:V], xe[:, 0:2576].indirect(T.JL[:, lo // 16:160]), XEk + ["JL"], tab("XE" + to, b0, 16))
                cp(T["FN" + to][:, lo:V], fn[:, 0:2576].indirect(T.JL[:, lo // 16:160]), FNk + ["JL"], tab("FN" + to, b0, 16))
                cur, nxt = nxt, cur
        else:
            for q in (3, 2, 1, 0):
                cp(xe[:, lo:W].indirect(l3(t, q, 0, 4)), l1(t, q), [("L1", t, q), ("L3", t, q)], wx)
            keep_sizes(t)
            store_names(t)
            dma("y", "d_yn", [lambda: g.sync.dma_start(T.yn[:], T.NBN[:, 0:V])], NB, ())
            store_sizes(t)
            dma("y", "d_yx", [lambda: g.sync.dma_start(T.yx[:], T.XSN[:, 16:2576])], XS, ())
            xo, xk = T["XE" + nxt], "XE" + nxt
            act(xo[:, 0:1280], xe[:, 0:2576].indirect(T.JL[:, 0:80]), XEk + ["JL"], tab(xk, 0, 8))
            cp(xo[:, 1280:V], xe[:, 0:2576].indirect(T.JL[:, 80:160]), XEk + ["JL"], tab(xk, 8, 16))
            for j, (a, b) in enumerate(((0, 480), (480, 960), (960, 1280), (1280, 1760), (1760, 2240), (2240, 2560))):
                bank = ("pN0", "pN1", "pM", "pW", "pD", "pE")[j]
                act(T.SGN[:, a:b], xo[:, a:b], tab(xk, a // 160, b // 160), [("SGN", j)] + (["SGN"] if j == 0 else []), func=F.Sign)
                op("t", mm(T[bank][:, 0:b - a], T.GN[:], T.SGN[:, a:b], True, True), ["GN", ("SGN", j)], [bank])
                for p in range(a, b, 160):
                    c = 15 - p // 160
                    tt(T.YJ[:, c:V:16], T[bank][:, p - a:p - a + 160], T.NU[:, c:V:16], A.max, [bank, "NU"], [("YJ", c)])
            dma("y", "d_yj", [lambda i=i: g.sync.dma_start(T.yj[i:i + 1, :], T.YJ[16 * i:16 * i + 1, :]) for i in range(8)], [("YJ", c) for c in M16], ())
    finish([("lo", nsend[0])])
